import numpy as np
import ml_dtypes


def mxq(x, axis, fmt="e4m3"):
    dtype, down = {"e4m3": (ml_dtypes.float8_e4m3fn, 7), "e5m2": (ml_dtypes.float8_e5m2, 14)}[fmt]
    v = np.moveaxis(np.asarray(x, np.float32).astype(ml_dtypes.bfloat16).astype(np.float64), axis, -1)
    blocks = v.reshape(v.shape[:-1] + (-1, 32))
    amax = np.abs(blocks).max(-1, keepdims=True)
    byte = np.maximum(np.where(amax > 0, np.frexp(amax)[1] - 1 + 127, 0) - down, 1)
    scale = np.exp2(byte - 127.0)
    codes = (blocks / scale).astype(np.float32).astype(dtype).astype(np.float64)
    return np.moveaxis((codes * scale).reshape(v.shape), -1, axis)


WIDE = False


def mx_kscale(k):
    if not WIDE:
        return np.ones(k)
    levels = np.array([10, -10, 5, -5, 0])
    if k % 512:
        return np.exp2(np.random.permutation(np.resize(levels, k // 32))).repeat(32)
    a = np.empty((k // 512, 16))
    for p in range(k // 512):
        a[p, :8] = np.random.permutation(np.resize(levels, 8))
        for g in range(8):
            far = levels[np.abs(levels - a[p, g]) >= 10]
            a[p, g + 8] = far[np.random.randint(len(far))]
    return np.exp2(a.ravel()).repeat(32)


def f64(x):
    return np.asarray(x).astype(np.float64)


def striped(idx):
    return np.tile(idx.reshape(-1, 16).T, (8, 1)).astype(np.uint16)


def unstriped(offs):
    return offs[:16].T.reshape(-1).astype(np.int64)


def striped8(idx):
    return np.concatenate([x.reshape(-1, 16).T for x in idx]).astype(np.uint16)


def runs(offs, k):
    lists = np.stack([offs[16 * r : 16 * r + 16].T.reshape(-1) for r in range(8)]).astype(np.int64)
    return lists[np.arange(k) % 512 // 64]


def pack_weight(w):
    k, n = w.shape
    w = f64(np.asarray(w, np.float32).astype(ml_dtypes.bfloat16)).reshape(k // 32, 32, n)
    amax = np.abs(w).max(1)
    byte = np.clip(np.where(amax > 0, np.frexp(amax)[1] - 1 + 127 - 7, 1), 1, 254)
    scaled = (w * np.exp2(127.0 - byte)[:, None, :]).reshape(k, n).astype(np.float32)
    words = np.ascontiguousarray(scaled.reshape(k // 512, 128, 4, n).transpose(0, 1, 3, 2)).astype(ml_dtypes.float8_e4m3fn).view(np.uint8)
    return words, np.ascontiguousarray(byte.astype(np.uint8).reshape(k // 512, 16, n))


def unpack_weight(words, scales):
    g, p, n, _ = words.shape
    vals = np.ascontiguousarray(words).view(ml_dtypes.float8_e4m3fn).astype(np.float64) * np.repeat(np.exp2(scales.astype(np.float64) - 127.0), 8, axis=1)[..., None]
    return vals.transpose(0, 1, 3, 2).reshape(g * 512, n)


def sigmoid(v):
    return 1.0 / (1.0 + np.exp(-np.maximum(v, -700.0)))


K, T, S, N, H, U = 512, 2048, 512, 512, 512, 1024


def setup_inputs():
    n = np.random.standard_normal
    s = mx_kscale(K)[:, None]
    u = mx_kscale(H)
    packed_xT = pack_weight(n((K, T)) * s)
    return {
        "x_words": packed_xT[0],
        "x_scales": packed_xT[1],
        "w1": (n((K, H)) / np.sqrt(K) / s).astype(np.float32),
        "w2": (n((K, H)) / np.sqrt(K) / s).astype(np.float32),
        "bw1": np.repeat(np.random.uniform(0.2, 1.0, (8, S)), 64, axis=0).astype(np.float32),
        "bw2": np.repeat(np.random.uniform(0.2, 1.0, (8, S)), 64, axis=0).astype(np.float32),
        "bw3": np.repeat(np.random.uniform(0.2, 1.0, (8, S)), 64, axis=0).astype(np.float32),
        "gn": (np.random.uniform(0.5, 1.5, (H, 1)) * u[:, None]).astype(np.float32),
        "w3": (n((H, N)) / np.sqrt(H) / u[:, None]).astype(np.float32),
        "mem": n((N, U)).astype(np.float32),
        "offs": striped(np.random.permutation(T)[:S]),
        "two": striped(np.random.permutation(T)[:S]),
        "v1": striped8(np.random.randint(0, S, (8, S))),
        "v2": striped8(np.random.randint(0, S, (8, S))),
        "v3": striped8(np.random.randint(0, S, (8, S))),
        "slot": striped8(np.stack([np.random.permutation(U)[:S] for _ in range(8)])),
    }


def reference(x_words, x_scales, w1, w2, bw1, bw2, bw3, gn, w3, mem, offs, two, v1, v2, v3, slot):
    x_two = unpack_weight(x_words, x_scales)[:, unstriped(two)]
    c = sigmoid(mxq(f64(w2), 0, "e4m3").T @ x_two)
    i1 = f64(bw1) / (c[np.arange(H)[:, None], runs(v1, H)] + 0.25)
    xq = unpack_weight(x_words, x_scales)[:, unstriped(offs)]
    y = mxq(f64(w1), 0, "e4m3").T @ xq
    i2 = f64(bw2) / (c[np.arange(H)[:, None], runs(v2, H)] + 0.25)
    i3 = f64(bw3) / (c[np.arange(H)[:, None], runs(v3, H)] + 0.25)
    z = f64(gn) * ((i1 * (y[np.arange(H)[:, None], runs(v1, H)]) + i2 * (y[np.arange(H)[:, None], runs(v2, H)]) + i3 * (y[np.arange(H)[:, None], runs(v3, H)])) / (i1 + i2 + i3))
    h = mxq(f64(w3), 0, "e4m3").T @ mxq(z, 0, "e4m3")
    out = f64(mem).copy()
    out[np.arange(N)[:, None], runs(slot, N)] = h
    return out

@@ -1,0 +1,269 @@
+import math
+from contextlib import ExitStack
+
+import concourse.mybir as mybir
+from concourse.masks import make_identity
+
+K, T, S, H, N, U = 512, 2048, 512, 512, 512, 1024
+FLOPS = 2 * K * H * S * 2 + 2 * H * N * S
+
+F32 = mybir.dt.float32
+BF16 = mybir.dt.bfloat16
+I32 = mybir.dt.int32
+U32 = mybir.dt.uint32
+U16 = mybir.dt.uint16
+U8 = mybir.dt.uint8
+FP8X4 = mybir.dt.float8_e4m3fn_x4
+ACT = mybir.ActivationFunctionType
+ALU = mybir.AluOpType
+
+P = 128
+PACK = 4
+CORNERS = 3
+HALF = S // 2
+HALF_COLS = HALF // 16
+BYTES = K * T + 16 * T + 4 * (2 * K * H + H * N + 3 * 8 * S + H + 2 * N * U) + 6 * P * 32 * 2
+
+
+def tile_picked_persp3_none_p_kernel(
+    tc, x_words, x_scales, w1, w2, bw1, bw2, bw3, gn, w3, mem, offs, two, v1, v2, v3, slot, out
+):
+    nc = tc.nc
+    with ExitStack() as ctx:
+        keep = ctx.enter_context(tc.tile_pool(name="keep", bufs=1))
+        ring = ctx.enter_context(tc.tile_pool(name="ring", bufs=4))
+        psum = ctx.enter_context(tc.psum_pool(name="psum", bufs=1))
+
+        def bank(index, shape, name):
+            return psum.tile(shape, F32, name=name, tag=f"bank{index}")
+
+        def load_list(source, name):
+            tile = keep.tile([P, S // 16], U16, name=name)
+            nc.sync.dma_start(tile[:], source)
+            return tile
+
+        def load_weight(source, name):
+            tile = keep.tile([P, PACK, 512], F32, name=name)
+            nc.sync.dma_start(out=tile[:], in_=source.rearrange("(p j) c -> p j c", j=PACK))
+            return tile
+
+        def load_quarter(source, name):
+            tile = keep.tile([P, S], F32, name=name)
+            nc.sync.dma_start(out=tile[:], in_=source.rearrange("(p t) c -> p t c", t=PACK)[:, 0, :])
+            return tile
+
+        warm = keep.tile([P, 1], F32, name="warm")
+        nc.vector.memset(warm[:], 0.0)
+        warmed = keep.tile([P, 1], F32, name="warmed")
+        nc.scalar.activation(warmed[:], warm[:], ACT.Sigmoid)
+
+        x_bytes = keep.tile([P, T], U8, name="x_bytes", align_bytes=64)
+        nc.gpsimd.memset(x_bytes[:].bitcast(I32), 0)
+        for q in range(4):
+            nc.sync.dma_start(
+                out=x_bytes[32 * q : 32 * q + 4, :].bitcast(I32),
+                in_=x_scales[0, 4 * q : 4 * q + 4, :].bitcast(I32),
+            )
+        two_list = load_list(two, "two_list")
+        offs_list = load_list(offs, "offs_list")
+        x_codes = keep.tile([P, T], I32, name="x_codes", align_bytes=64)
+        nc.sync.dma_start(out=x_codes[:], in_=x_words[0].rearrange("p n t -> p (n t)").bitcast(I32))
+        w2_raw = load_weight(w2, "w2_raw")
+        w1_raw = load_weight(w1, "w1_raw")
+        corner_lists = [load_list(v, f"corner_list{k}") for k, v in enumerate((v1, v2, v3))]
+        gain = keep.tile([P, PACK], F32, name="gain")
+        nc.sync.dma_start(out=gain[:], in_=gn.rearrange("(p t) o -> p (t o)", t=PACK))
+        bary = [load_quarter(b, f"bary{k}") for k, b in enumerate((bw1, bw2, bw3))]
+        w3_raw = load_weight(w3, "w3_raw")
+        slot_list = load_list(slot, "slot_list")
+        pages = []
+        for t in range(PACK):
+            page = keep.tile([P, U], F32, name=f"page{t}")
+            nc.sync.dma_start(out=page[:], in_=mem.rearrange("(p t) c -> p t c", t=PACK)[:, t, :])
+            pages.append(page)
+        ident = keep.tile([P, P], F32, name="ident")
+        make_identity(nc, ident[:])
+
+        def pick_bytes(offsets, name):
+            tile = keep.tile([P, S], U8, name=name, align_bytes=64)
+            nc.vector.tensor_copy(tile[:], x_bytes[:].indirect(offsets[:]))
+            return tile
+
+        def pick_words(offsets, name):
+            tile = keep.tile([P, S], U32, name=name, align_bytes=64)
+            nc.vector.tensor_copy(tile[:], x_codes[:].bitcast(U32).indirect(offsets[:]))
+            return tile
+
+        two_bytes = pick_bytes(two_list, "two_bytes")
+        offs_bytes = pick_bytes(offs_list, "offs_bytes")
+        two_words = pick_words(two_list, "two_words")
+        offs_words = pick_words(offs_list, "offs_words")
+
+        def weave(raw, pair, name, copy):
+            tile = keep.tile([P, 2, P, PACK], BF16, name=name, align_bytes=64)
+            copy(
+                tile[:].rearrange("p t m j -> p m t j"),
+                raw[:].rearrange("p j (m t) -> p m t j", t=PACK)[:, :, 2 * pair : 2 * pair + 2, :],
+            )
+            return tile
+
+        def quantise(woven, name):
+            width = woven.shape[1] * woven.shape[2]
+            codes = keep.tile([P, width], U32, name=f"{name}_codes", align_bytes=64)
+            scales = keep.tile([P, width], U8, name=f"{name}_scales", align_bytes=64)
+            nc.vector.quantize_mx(
+                out=codes[:].bitcast(FP8X4), scales=scales[:], in_=woven[:].rearrange("p a b j -> p (a b j)")
+            )
+            return codes, scales
+
+        def product(acc, pairs, t, words, scale_bytes):
+            codes, scales = pairs[t // 2]
+            cols = slice((t % 2) * P, (t % 2 + 1) * P)
+            nc.tensor.matmul_mx(
+                out=acc,
+                lhsT=codes[:, cols].bitcast(FP8X4),
+                lhsT_scale=scales[:, cols],
+                rhs=words.bitcast(FP8X4),
+                rhs_scale=scale_bytes,
+                start=True,
+                stop=True,
+            )
+
+        w2_woven = [weave(w2_raw, 0, "w2_woven0", nc.vector.tensor_copy), weave(w2_raw, 1, "w2_woven1", nc.scalar.copy)]
+        w2_mx = [quantise(w2_woven[pair], f"w2_{pair}") for pair in range(2)]
+        logits = []
+        for t in range(PACK):
+            acc = bank(t, [P, S], f"depth_acc{t}")
+            product(acc[:], w2_mx, t, two_words[:], two_bytes[:])
+            logit = keep.tile([P, S], F32, name=f"logit{t}")
+            nc.scalar.activation(logit[:], acc[:], ACT.Copy, scale=-1.0, bias=-math.log(5.0))
+            logits.append(logit)
+
+        w1_woven = [weave(w1_raw, pair, f"w1_woven{pair}", nc.vector.tensor_copy) for pair in range(2)]
+        w1_mx = [quantise(w1_woven[pair], f"w1_{pair}") for pair in range(2)]
+        attrs = []
+        for t in range(PACK):
+            acc = bank(PACK + t, [P, S], f"attr_acc{t}")
+            product(acc[:], w1_mx, t, offs_words[:], offs_bytes[:])
+            attr = keep.tile([P, S], F32, name=f"attr{t}")
+            nc.scalar.activation(attr[:], acc[:], ACT.Copy, scale=gain[:, t : t + 1])
+            attrs.append(attr)
+
+        steps = [(h, t, k) for h in range(2) for t in range(PACK) for k in range(CORNERS)]
+        den = [bank(b, [P, PACK, P], f"den{b}") for b in range(4)]
+        num = [bank(PACK + b, [P, PACK, P], f"num{b}") for b in range(4)]
+        den_sq = keep.tile([P, 4, 2, P, 2], F32, name="den_sq")
+
+        def by_word(acc):
+            return acc[:].rearrange("s (u e) p -> s u p e", e=2)
+
+        def add_turned(sums, h, t, k, values):
+            for b in range(2):
+                nc.tensor.matmul(
+                    sums[2 * h + b][:, t, :],
+                    values[:, b * P : (b + 1) * P],
+                    ident[:],
+                    is_transpose=True,
+                    start=(k == 0),
+                    stop=(k == CORNERS - 1),
+                )
+
+        weights = []
+
+        def weigh(n):
+            h, t, k = steps[n]
+            offsets = corner_lists[k][:, h * HALF_COLS : (h + 1) * HALF_COLS]
+            sig = keep.tile([P, HALF], F32, name=f"sig{n}")
+            nc.scalar.activation(sig[:], logits[t][:].indirect(offsets), ACT.Sigmoid)
+            weight = keep.tile([P, HALF], F32, name=f"weight{n}")
+            nc.vector.scalar_tensor_tensor(
+                weight[:], sig[:], 0.25, bary[k][:, h * HALF : (h + 1) * HALF], ALU.add, ALU.mult
+            )
+            weights.append(weight)
+            add_turned(den, h, t, k, weight)
+            if t == PACK - 1 and k == CORNERS - 1:
+                for b in range(2 * h, 2 * h + 2):
+                    nc.scalar.activation(den_sq[:, b], by_word(den[b]), ACT.Square)
+
+        for n, (h, t, k) in enumerate(steps):
+            while len(weights) < min(len(steps), 2 + (3 * n) // 2):
+                weigh(len(weights))
+            offsets = corner_lists[k][:, h * HALF_COLS : (h + 1) * HALF_COLS]
+            term = ring.tile([P, HALF], F32, name="term")
+            nc.vector.tensor_tensor(term[:], attrs[t][:].indirect(offsets), weights[n][:], ALU.mult)
+            add_turned(num, h, t, k, term)
+
+        den_log = keep.tile([P, 4, S], F32, name="den_log")
+        nc.scalar.activation(
+            den_log[:].rearrange("s b c -> s (b c)"), den_sq[:].rearrange("s b u p e -> s (b u p e)"), ACT.Ln
+        )
+        inv_sq = []
+        for b in range(4):
+            tile = keep.tile([P, 2, P, 2], F32, name=f"inv_sq{b}")
+            nc.scalar.activation(tile[:].rearrange("s u p e -> s (u p e)"), den_log[:, b, :], ACT.Exp, scale=-1.0)
+            inv_sq.append(tile)
+
+        w3_woven = [weave(w3_raw, pair, f"w3_woven{pair}", nc.vector.tensor_copy) for pair in range(2)]
+        w3_mx = [quantise(w3_woven[pair], f"w3_{pair}") for pair in range(2)]
+
+        inv = {}
+        z_rows = {}
+        z_woven = {}
+        results = {}
+
+        def invert(b):
+            tile = keep.tile([P, 2, P, 2], F32, name=f"inv{b}")
+            nc.vector.tensor_tensor(tile[:], by_word(den[b]), inv_sq[b][:], ALU.mult)
+            inv[b] = tile
+
+        def divide(b):
+            tile = keep.tile([P, 2, P, 2], BF16, name=f"z_rows{b}")
+            nc.vector.tensor_tensor(tile[:], by_word(num[b]), inv[b][:], ALU.mult)
+            z_rows[b] = tile
+
+        def turn_back(h):
+            acc = bank(2 * h, [P, 2, 2, P], f"z_acc{h}")
+            for b in range(2):
+                words = z_rows[2 * h + b][:].rearrange("s u p e -> s (u p e)").bitcast(F32)
+                for u in range(2):
+                    nc.tensor.transpose(acc[:, b, u, :], words[:, u * P : (u + 1) * P], ident[:])
+            tile = keep.tile([P, 2, P, PACK], BF16, name=f"z_woven{h}", align_bytes=64)
+            nc.scalar.copy(
+                tile[:].rearrange("p b s j -> p (b s j)").bitcast(F32).rearrange("p (b s u) -> p b s u", b=2, u=2),
+                acc[:].rearrange("p b u s -> p b s u"),
+            )
+            z_woven[h] = tile
+
+        def project(h):
+            codes, scales = quantise(z_woven[h], f"z_{h}")
+            banks = (2 * h + 1, PACK + 2 * h, PACK + 2 * h + 1, 2 * h)
+            for t in range(PACK):
+                acc = bank(banks[t], [P, HALF], f"out_acc{h}_{t}")
+                product(acc[:], w3_mx, t, codes[:], scales[:])
+                tile = keep.tile([P, HALF], F32, name=f"result{h}_{t}")
+                nc.scalar.copy(tile[:], acc[:])
+                results[h, t] = tile
+
+        def put(h, t):
+            offsets = slot_list[:, h * HALF_COLS : (h + 1) * HALF_COLS]
+            nc.vector.tensor_copy(pages[t][:].indirect(offsets), results[h, t][:])
+            if h == 1:
+                nc.sync.dma_start(out=out.rearrange("(p t) c -> p t c", t=PACK)[:, t, :], in_=pages[t][:])
+
+        invert(0)
+        invert(1)
+        divide(0)
+        divide(1)
+        turn_back(0)
+        invert(2)
+        invert(3)
+        divide(2)
+        project(0)
+        divide(3)
+        turn_back(1)
+        put(0, 0)
+        project(1)
+        for t in range(1, PACK):
+            put(0, t)
+            put(1, t - 1)
+        put(1, PACK - 1)

@@ -31,7 +31,7 @@ def tile_picked_persp3_none_p_kernel(
     nc = tc.nc
     with ExitStack() as ctx:
         keep = ctx.enter_context(tc.tile_pool(name="keep", bufs=1))
-        ring = ctx.enter_context(tc.tile_pool(name="ring", bufs=4))
+        ring = ctx.enter_context(tc.tile_pool(name="ring", bufs=8))
         psum = ctx.enter_context(tc.psum_pool(name="psum", bufs=1))
 
         def bank(index, shape, name):
@@ -43,9 +43,13 @@ def tile_picked_persp3_none_p_kernel(
             return tile
 
         def load_weight(source, name):
-            tile = keep.tile([P, PACK, 512], F32, name=name)
-            nc.sync.dma_start(out=tile[:], in_=source.rearrange("(p j) c -> p j c", j=PACK))
-            return tile
+            halves = []
+            for half in range(2):
+                tile = keep.tile([P, PACK, 256], F32, name=f"{name}{half}", tag=f"{name}{half}", align_bytes=64)
+                rows = source.rearrange("(p j) c -> p j c", j=PACK)
+                nc.sync.dma_start(out=tile[:], in_=rows[:, :, half * 256 : (half + 1) * 256])
+                halves.append(tile)
+            return halves
 
         def load_quarter(source, name):
             tile = keep.tile([P, S], F32, name=name)
@@ -69,11 +73,13 @@ def tile_picked_persp3_none_p_kernel(
         x_codes = keep.tile([P, T], I32, name="x_codes", align_bytes=64)
         nc.sync.dma_start(out=x_codes[:], in_=x_words[0].rearrange("p n t -> p (n t)").bitcast(I32))
         w2_raw = load_weight(w2, "w2_raw")
-        w1_raw = load_weight(w1, "w1_raw")
-        corner_lists = [load_list(v, f"corner_list{k}") for k, v in enumerate((v1, v2, v3))]
-        gain = keep.tile([P, PACK], F32, name="gain")
+        gain = keep.tile([P, PACK], F32, name="gain", tag="gain", align_bytes=64)
         nc.sync.dma_start(out=gain[:], in_=gn.rearrange("(p t) o -> p (t o)", t=PACK))
-        bary = [load_quarter(b, f"bary{k}") for k, b in enumerate((bw1, bw2, bw3))]
+        w1_raw = load_weight(w1, "w1_raw")
+        corner_lists = [load_list(v1, "corner_list0")]
+        bary = [load_quarter(bw1, "bary0")]
+        corner_lists += [load_list(v2, "corner_list1"), load_list(v3, "corner_list2")]
+        bary += [load_quarter(bw2, "bary1"), load_quarter(bw3, "bary2")]
         w3_raw = load_weight(w3, "w3_raw")
         slot_list = load_list(slot, "slot_list")
         pages = []
@@ -81,6 +87,16 @@ def tile_picked_persp3_none_p_kernel(
             page = keep.tile([P, U], F32, name=f"page{t}")
             nc.sync.dma_start(out=page[:], in_=mem.rearrange("(p t) c -> p t c", t=PACK)[:, t, :])
             pages.append(page)
+        def window(t, name, memset):
+            if t == PACK - 1:
+                return keep.tile([P, S], F32, name=name, tag=name, align_bytes=64)
+            tile = keep.tile([P, 2 * S], F32, name=name)
+            memset(tile[:, S:], 0.0)
+            return tile
+
+        logits = [window(t, f"logit{t}", nc.gpsimd.memset) for t in range(PACK)]
+        attrs = [window(t, f"attr{t}", nc.vector.memset) for t in range(PACK)]
+
         ident = keep.tile([P, P], F32, name="ident")
         make_identity(nc, ident[:])
 
@@ -99,20 +115,18 @@ def tile_picked_persp3_none_p_kernel(
         two_words = pick_words(two_list, "two_words")
         offs_words = pick_words(offs_list, "offs_words")
 
-        def weave(raw, pair, name, copy):
-            tile = keep.tile([P, 2, P, PACK], BF16, name=name, align_bytes=64)
+        def weave(raw, woven, half, copy):
             copy(
-                tile[:].rearrange("p t m j -> p m t j"),
-                raw[:].rearrange("p j (m t) -> p m t j", t=PACK)[:, :, 2 * pair : 2 * pair + 2, :],
+                woven[:, :, half * 64 : (half + 1) * 64, :].rearrange("p t m j -> p m t j"),
+                raw[half][:].rearrange("p j (m t) -> p m t j", t=PACK),
             )
-            return tile
 
         def quantise(woven, name):
             width = woven.shape[1] * woven.shape[2]
             codes = keep.tile([P, width], U32, name=f"{name}_codes", align_bytes=64)
             scales = keep.tile([P, width], U8, name=f"{name}_scales", align_bytes=64)
             nc.vector.quantize_mx(
-                out=codes[:].bitcast(FP8X4), scales=scales[:], in_=woven[:].rearrange("p a b j -> p (a b j)")
+                out=codes[:].bitcast(FP8X4), scales=scales[:], in_=woven.rearrange("p a b j -> p (a b j)")
             )
             return codes, scales
 
@@ -129,91 +143,129 @@ def tile_picked_persp3_none_p_kernel(
                 stop=True,
             )
 
-        w2_woven = [weave(w2_raw, 0, "w2_woven0", nc.vector.tensor_copy), weave(w2_raw, 1, "w2_woven1", nc.scalar.copy)]
-        w2_mx = [quantise(w2_woven[pair], f"w2_{pair}") for pair in range(2)]
-        logits = []
+        def quantise_weight(woven, name):
+            return [quantise(woven[:, 2 * pair : 2 * pair + 2], f"{name}_{pair}") for pair in range(2)]
+
+        woven = {name: keep.tile([P, PACK, P, PACK], BF16, name=f"{name}_woven", tag=f"{name}_woven", align_bytes=64) for name in ("w1", "w2")}
+        weave(w2_raw, woven["w2"], 0, nc.scalar.copy)
+        weave(w2_raw, woven["w2"], 1, nc.vector.tensor_copy)
+        w2_mx = quantise_weight(woven["w2"], "w2")
         for t in range(PACK):
             acc = bank(t, [P, S], f"depth_acc{t}")
             product(acc[:], w2_mx, t, two_words[:], two_bytes[:])
-            logit = keep.tile([P, S], F32, name=f"logit{t}")
-            nc.scalar.activation(logit[:], acc[:], ACT.Copy, scale=-1.0, bias=-math.log(5.0))
-            logits.append(logit)
+            if t == 0:
+                first_sig = keep.tile([P, S], F32, name="first_sig")
+                nc.scalar.activation(first_sig[:], acc[:], ACT.Sigmoid, scale=-1.0, bias=-math.log(5.0))
+                nc.scalar.activation(logits[0][:, :S], first_sig[:], ACT.Copy, bias=0.25)
+            else:
+                nc.scalar.activation(logits[t][:, :S], acc[:], ACT.Copy, scale=-1.0, bias=-math.log(5.0))
 
-        w1_woven = [weave(w1_raw, pair, f"w1_woven{pair}", nc.vector.tensor_copy) for pair in range(2)]
-        w1_mx = [quantise(w1_woven[pair], f"w1_{pair}") for pair in range(2)]
-        attrs = []
-        for t in range(PACK):
-            acc = bank(PACK + t, [P, S], f"attr_acc{t}")
-            product(acc[:], w1_mx, t, offs_words[:], offs_bytes[:])
-            attr = keep.tile([P, S], F32, name=f"attr{t}")
-            nc.scalar.activation(attr[:], acc[:], ACT.Copy, scale=gain[:, t : t + 1])
-            attrs.append(attr)
-
-        steps = [(h, t, k) for h in range(2) for t in range(PACK) for k in range(CORNERS)]
-        den = [bank(b, [P, PACK, P], f"den{b}") for b in range(4)]
-        num = [bank(PACK + b, [P, PACK, P], f"num{b}") for b in range(4)]
-        den_sq = keep.tile([P, 4, 2, P, 2], F32, name="den_sq")
+        steps = [(range(4), t, k) for t in range(PACK - 1) for k in range(CORNERS)]
+        steps += [(range(2 * h, 2 * h + 2), PACK - 1, k) for h in range(2) for k in range(CORNERS)]
+        den = []
+        den_sq = [keep.tile([P, 2, 2, P, 2], F32, name=f"den_sq{h}", tag=f"den_sq{h}") for h in range(2)]
 
         def by_word(acc):
             return acc[:].rearrange("s (u e) p -> s u p e", e=2)
 
-        def add_turned(sums, h, t, k, values):
-            for b in range(2):
+        def add_turned(sums, blocks, t, k, values):
+            for place, b in enumerate(blocks):
                 nc.tensor.matmul(
-                    sums[2 * h + b][:, t, :],
-                    values[:, b * P : (b + 1) * P],
+                    sums[b][:, t, :],
+                    values[:, place * P : (place + 1) * P],
                     ident[:],
                     is_transpose=True,
                     start=(k == 0),
                     stop=(k == CORNERS - 1),
                 )
 
+        def square(h):
+            for b in range(2):
+                nc.scalar.activation(den_sq[h][:, b], by_word(den[2 * h + b]), ACT.Square)
+
         weights = []
+        sigs = []
 
         def weigh(n):
-            h, t, k = steps[n]
-            offsets = corner_lists[k][:, h * HALF_COLS : (h + 1) * HALF_COLS]
-            sig = keep.tile([P, HALF], F32, name=f"sig{n}")
-            nc.scalar.activation(sig[:], logits[t][:].indirect(offsets), ACT.Sigmoid)
-            weight = keep.tile([P, HALF], F32, name=f"weight{n}")
-            nc.vector.scalar_tensor_tensor(
-                weight[:], sig[:], 0.25, bary[k][:, h * HALF : (h + 1) * HALF], ALU.add, ALU.mult
-            )
+            blocks, t, k = steps[n]
+            width = len(blocks) * P
+            offsets = corner_lists[k][:, blocks.start * 8 : blocks.stop * 8]
+            weight = keep.tile([P, width], F32, name=f"weight{n}", tag="w1_raw1" if n == 0 else f"weight{n}", align_bytes=64)
+            if t == 0:
+                nc.vector.tensor_tensor(weight[:], logits[0][:].indirect(offsets), bary[k][:], ALU.mult)
+            else:
+                if n <= CORNERS + 1:
+                    columns = S if n == CORNERS else (2 * CORNERS + 2) * S
+                    tag = "early_sig" if n == CORNERS else "gain"
+                    sigs.append(keep.tile([P, columns], F32, name=f"sigs{n}", tag=tag, align_bytes=64))
+                start = sum(w.shape[1] for w in weights[CORNERS + 1 :])
+                sig = sigs[-1][:, start : start + width]
+                nc.scalar.activation(sig, logits[t][:].indirect(offsets), ACT.Sigmoid)
+                nc.vector.scalar_tensor_tensor(
+                    weight[:], sig, 0.25, bary[k][:, blocks.start * P : blocks.stop * P], ALU.add, ALU.mult
+                )
             weights.append(weight)
-            add_turned(den, h, t, k, weight)
-            if t == PACK - 1 and k == CORNERS - 1:
-                for b in range(2 * h, 2 * h + 2):
-                    nc.scalar.activation(den_sq[:, b], by_word(den[b]), ACT.Square)
+            if n > 0:
+                add_turned(den, blocks, t, k, weight)
+            if n == len(steps) - 2:
+                square(0)
 
-        for n, (h, t, k) in enumerate(steps):
-            while len(weights) < min(len(steps), 2 + (3 * n) // 2):
+        for half in range(2):
+            weave(w1_raw, woven["w1"], half, nc.vector.tensor_copy)
+        weigh(0)
+        w1_mx = quantise_weight(woven["w1"], "w1")
+        for t in range(PACK):
+            acc = bank(PACK + t, [P, S], f"attr_acc{t}")
+            product(acc[:], w1_mx, t, offs_words[:], offs_bytes[:])
+            nc.scalar.activation(attrs[t][:, :S], acc[:], ACT.Copy, scale=gain[:, t : t + 1])
+        den += [bank(PACK + b, [P, PACK, P], f"den{b}") for b in range(4)]
+        num = [bank(b, [P, PACK, P], f"num{b}") for b in range(4)]
+        add_turned(den, *steps[0], weights[0])
+
+        def add_term(n, term):
+            blocks, t, k = steps[n]
+            offsets = corner_lists[k][:, blocks.start * 8 : blocks.stop * 8]
+            nc.vector.tensor_tensor(term, attrs[t][:].indirect(offsets), weights[n][:], ALU.mult)
+            add_turned(num, blocks, t, k, term)
+
+        for n in range(len(steps) - CORNERS):
+            while len(weights) < len(steps) and sum(w.shape[1] for w in weights) < S * (3 + 2 * n):
                 weigh(len(weights))
-            offsets = corner_lists[k][:, h * HALF_COLS : (h + 1) * HALF_COLS]
-            term = ring.tile([P, HALF], F32, name="term")
-            nc.vector.tensor_tensor(term[:], attrs[t][:].indirect(offsets), weights[n][:], ALU.mult)
-            add_turned(num, h, t, k, term)
+            term = ring.tile([P, weights[n].shape[1]], F32, name="term")
+            add_term(n, term[:])
 
-        den_log = keep.tile([P, 4, S], F32, name="den_log")
-        nc.scalar.activation(
-            den_log[:].rearrange("s b c -> s (b c)"), den_sq[:].rearrange("s b u p e -> s (b u p e)"), ACT.Ln
-        )
+        den_log = []
+        for h in range(2):
+            if h == 1:
+                square(1)
+            tile = keep.tile([P, 2, S], F32, name=f"den_log{h}", tag="logit3" if h == 0 else "den_log1", align_bytes=64)
+            nc.scalar.activation(
+                tile[:].rearrange("s b c -> s (b c)"), den_sq[h][:].rearrange("s b u p e -> s (b u p e)"), ACT.Ln
+            )
+            den_log.append(tile)
         inv_sq = []
-        for b in range(4):
-            tile = keep.tile([P, 2, P, 2], F32, name=f"inv_sq{b}")
-            nc.scalar.activation(tile[:].rearrange("s u p e -> s (u p e)"), den_log[:, b, :], ACT.Exp, scale=-1.0)
+        for h in range(2):
+            if h == 1:
+                w3_woven = keep.tile([P, PACK, P, PACK], BF16, name="w3_woven", tag="logit3", align_bytes=64)
+                for half in range(2):
+                    weave(w3_raw, w3_woven, half, nc.scalar.copy)
+            tile = keep.tile([P, 2, 2, P, 2], F32, name=f"inv_sq{h}", tag="den_sq1" if h == 0 else "inv_sq1")
+            for b in range(2):
+                nc.scalar.activation(
+                    tile[:, b].rearrange("s u p e -> s (u p e)"), den_log[h][:, b, :], ACT.Exp, scale=-1.0
+                )
             inv_sq.append(tile)
 
-        w3_woven = [weave(w3_raw, pair, f"w3_woven{pair}", nc.vector.tensor_copy) for pair in range(2)]
-        w3_mx = [quantise(w3_woven[pair], f"w3_{pair}") for pair in range(2)]
 
         inv = {}
         z_rows = {}
         z_woven = {}
         results = {}
+        sums = {}
 
         def invert(b):
-            tile = keep.tile([P, 2, P, 2], F32, name=f"inv{b}")
-            nc.vector.tensor_tensor(tile[:], by_word(den[b]), inv_sq[b][:], ALU.mult)
+            tile = keep.tile([P, 2, P, 2], F32, name=f"inv{b}", tag=f"inv{b}")
+            nc.vector.tensor_tensor(tile[:], by_word(den[b]), inv_sq[b // 2][:, b % 2], ALU.mult)
             inv[b] = tile
 
         def divide(b):
@@ -222,12 +274,12 @@ def tile_picked_persp3_none_p_kernel(
             z_rows[b] = tile
 
         def turn_back(h):
-            acc = bank(2 * h, [P, 2, 2, P], f"z_acc{h}")
+            acc = bank(PACK + 2 * h, [P, 2, 2, P], f"z_acc{h}")
             for b in range(2):
                 words = z_rows[2 * h + b][:].rearrange("s u p e -> s (u p e)").bitcast(F32)
                 for u in range(2):
                     nc.tensor.transpose(acc[:, b, u, :], words[:, u * P : (u + 1) * P], ident[:])
-            tile = keep.tile([P, 2, P, PACK], BF16, name=f"z_woven{h}", align_bytes=64)
+            tile = keep.tile([P, 2, P, PACK], BF16, name=f"z_woven{h}", tag=f"z_woven{h}", align_bytes=64)
             nc.scalar.copy(
                 tile[:].rearrange("p b s j -> p (b s j)").bitcast(F32).rearrange("p (b s u) -> p b s u", b=2, u=2),
                 acc[:].rearrange("p b u s -> p b s u"),
@@ -235,14 +287,18 @@ def tile_picked_persp3_none_p_kernel(
             z_woven[h] = tile
 
         def project(h):
-            codes, scales = quantise(z_woven[h], f"z_{h}")
-            banks = (2 * h + 1, PACK + 2 * h, PACK + 2 * h + 1, 2 * h)
+            codes, scales = quantise(z_woven[h][:], f"z_{h}")
+            banks = (PACK + 2 * h + 1, 2 * h, 2 * h + 1, PACK + 2 * h)
             for t in range(PACK):
                 acc = bank(banks[t], [P, HALF], f"out_acc{h}_{t}")
                 product(acc[:], w3_mx, t, codes[:], scales[:])
-                tile = keep.tile([P, HALF], F32, name=f"result{h}_{t}")
-                nc.scalar.copy(tile[:], acc[:])
-                results[h, t] = tile
+                sums[h, t] = acc
+
+        def take(h, t):
+            tag = "z_woven1" if (h, t) == (0, 1) else f"result{h}_{t}"
+            tile = keep.tile([P, HALF], F32, name=f"result{h}_{t}", tag=tag, align_bytes=64)
+            nc.scalar.copy(tile[:], sums[h, t][:])
+            results[h, t] = tile
 
         def put(h, t):
             offsets = slot_list[:, h * HALF_COLS : (h + 1) * HALF_COLS]
@@ -255,14 +311,23 @@ def tile_picked_persp3_none_p_kernel(
         divide(0)
         divide(1)
         turn_back(0)
+        last_terms = keep.tile([P, CORNERS, HALF], F32, name="last_terms", tag="inv1")
+        for k in range(CORNERS):
+            add_term(len(steps) - CORNERS + k, last_terms[:, k, :])
+        w3_mx = quantise_weight(w3_woven, "w3")
+        project(0)
+        take(0, 0)
         invert(2)
         invert(3)
         divide(2)
-        project(0)
         divide(3)
         turn_back(1)
         put(0, 0)
         project(1)
+        for t in range(1, PACK):
+            take(0, t)
+            take(1, t - 1)
+        take(1, PACK - 1)
         for t in range(1, PACK):
             put(0, t)
             put(1, t - 1)

@@ -56,11 +56,6 @@ def tile_picked_persp3_none_p_kernel(
             nc.sync.dma_start(out=tile[:], in_=source.rearrange("(p t) c -> p t c", t=PACK)[:, 0, :])
             return tile
 
-        warm = keep.tile([P, 1], F32, name="warm")
-        nc.vector.memset(warm[:], 0.0)
-        warmed = keep.tile([P, 1], F32, name="warmed")
-        nc.scalar.activation(warmed[:], warm[:], ACT.Sigmoid)
-
         x_bytes = keep.tile([P, T], U8, name="x_bytes", align_bytes=64)
         nc.gpsimd.memset(x_bytes[:].bitcast(I32), 0)
         for q in range(4):

import math
from contextlib import ExitStack

import concourse.mybir as mybir
from concourse.masks import make_identity

K, T, S, H, N, U = 512, 2048, 512, 512, 512, 1024
FLOPS = 2 * K * H * S * 2 + 2 * H * N * S

F32 = mybir.dt.float32
BF16 = mybir.dt.bfloat16
I32 = mybir.dt.int32
U32 = mybir.dt.uint32
U16 = mybir.dt.uint16
U8 = mybir.dt.uint8
FP8X4 = mybir.dt.float8_e4m3fn_x4
ACT = mybir.ActivationFunctionType
ALU = mybir.AluOpType

P = 128
PACK = 4
CORNERS = 3
HALF = S // 2
HALF_COLS = HALF // 16
BYTES = K * T + 16 * T + 4 * (2 * K * H + H * N + 3 * 8 * S + H + 2 * N * U) + 6 * P * 32 * 2


def tile_picked_persp3_none_p_kernel(
    tc, x_words, x_scales, w1, w2, bw1, bw2, bw3, gn, w3, mem, offs, two, v1, v2, v3, slot, out
):
    nc = tc.nc
    with ExitStack() as ctx:
        keep = ctx.enter_context(tc.tile_pool(name="keep", bufs=1))
        ring = ctx.enter_context(tc.tile_pool(name="ring", bufs=8))
        psum = ctx.enter_context(tc.psum_pool(name="psum", bufs=1))

        def bank(index, shape, name):
            return psum.tile(shape, F32, name=name, tag=f"bank{index}")

        def load_list(source, name):
            tile = keep.tile([P, S // 16], U16, name=name)
            nc.sync.dma_start(tile[:], source)
            return tile

        def load_weight(source, name):
            halves = []
            for half in range(2):
                tile = keep.tile([P, PACK, 256], F32, name=f"{name}{half}", tag=f"{name}{half}", align_bytes=64)
                rows = source.rearrange("(p j) c -> p j c", j=PACK)
                nc.sync.dma_start(out=tile[:], in_=rows[:, :, half * 256 : (half + 1) * 256])
                halves.append(tile)
            return halves

        def load_quarter(source, name):
            tile = keep.tile([P, S], F32, name=name)
            nc.sync.dma_start(out=tile[:], in_=source.rearrange("(p t) c -> p t c", t=PACK)[:, 0, :])
            return tile

        x_bytes = keep.tile([P, T], U8, name="x_bytes", align_bytes=64)
        nc.gpsimd.memset(x_bytes[:].bitcast(I32), 0)
        for q in range(4):
            nc.sync.dma_start(
                out=x_bytes[32 * q : 32 * q + 4, :].bitcast(I32),
                in_=x_scales[0, 4 * q : 4 * q + 4, :].bitcast(I32),
            )
        two_list = load_list(two, "two_list")
        offs_list = load_list(offs, "offs_list")
        x_codes = keep.tile([P, T], I32, name="x_codes", align_bytes=64)
        nc.sync.dma_start(out=x_codes[:], in_=x_words[0].rearrange("p n t -> p (n t)").bitcast(I32))
        w2_raw = load_weight(w2, "w2_raw")
        gain = keep.tile([P, PACK], F32, name="gain", tag="gain", align_bytes=64)
        nc.sync.dma_start(out=gain[:], in_=gn.rearrange("(p t) o -> p (t o)", t=PACK))
        w1_raw = load_weight(w1, "w1_raw")
        corner_lists = [load_list(v1, "corner_list0")]
        bary = [load_quarter(bw1, "bary0")]
        corner_lists += [load_list(v2, "corner_list1"), load_list(v3, "corner_list2")]
        bary += [load_quarter(bw2, "bary1"), load_quarter(bw3, "bary2")]
        w3_raw = load_weight(w3, "w3_raw")
        slot_list = load_list(slot, "slot_list")
        pages = []
        for t in range(PACK):
            page = keep.tile([P, U], F32, name=f"page{t}")
            nc.sync.dma_start(out=page[:], in_=mem.rearrange("(p t) c -> p t c", t=PACK)[:, t, :])
            pages.append(page)
        def window(t, name, memset):
            if t == PACK - 1:
                return keep.tile([P, S], F32, name=name, tag=name, align_bytes=64)
            tile = keep.tile([P, 2 * S], F32, name=name)
            memset(tile[:, S:], 0.0)
            return tile

        logits = [window(t, f"logit{t}", nc.gpsimd.memset) for t in range(PACK)]
        attrs = [window(t, f"attr{t}", nc.vector.memset) for t in range(PACK)]

        ident = keep.tile([P, P], F32, name="ident")
        make_identity(nc, ident[:])

        def pick_bytes(offsets, name):
            tile = keep.tile([P, S], U8, name=name, align_bytes=64)
            nc.vector.tensor_copy(tile[:], x_bytes[:].indirect(offsets[:]))
            return tile

        def pick_words(offsets, name):
            tile = keep.tile([P, S], U32, name=name, align_bytes=64)
            nc.vector.tensor_copy(tile[:], x_codes[:].bitcast(U32).indirect(offsets[:]))
            return tile

        two_bytes = pick_bytes(two_list, "two_bytes")
        offs_bytes = pick_bytes(offs_list, "offs_bytes")
        two_words = pick_words(two_list, "two_words")
        offs_words = pick_words(offs_list, "offs_words")

        def weave(raw, woven, half, copy):
            copy(
                woven[:, :, half * 64 : (half + 1) * 64, :].rearrange("p t m j -> p m t j"),
                raw[half][:].rearrange("p j (m t) -> p m t j", t=PACK),
            )

        def quantise(woven, name):
            width = woven.shape[1] * woven.shape[2]
            codes = keep.tile([P, width], U32, name=f"{name}_codes", align_bytes=64)
            scales = keep.tile([P, width], U8, name=f"{name}_scales", align_bytes=64)
            nc.vector.quantize_mx(
                out=codes[:].bitcast(FP8X4), scales=scales[:], in_=woven.rearrange("p a b j -> p (a b j)")
            )
            return codes, scales

        def product(acc, pairs, t, words, scale_bytes):
            codes, scales = pairs[t // 2]
            cols = slice((t % 2) * P, (t % 2 + 1) * P)
            nc.tensor.matmul_mx(
                out=acc,
                lhsT=codes[:, cols].bitcast(FP8X4),
                lhsT_scale=scales[:, cols],
                rhs=words.bitcast(FP8X4),
                rhs_scale=scale_bytes,
                start=True,
                stop=True,
            )

        def quantise_weight(woven, name):
            return [quantise(woven[:, 2 * pair : 2 * pair + 2], f"{name}_{pair}") for pair in range(2)]

        woven = {name: keep.tile([P, PACK, P, PACK], BF16, name=f"{name}_woven", tag=f"{name}_woven", align_bytes=64) for name in ("w1", "w2")}
        weave(w2_raw, woven["w2"], 0, nc.scalar.copy)
        weave(w2_raw, woven["w2"], 1, nc.vector.tensor_copy)
        w2_mx = quantise_weight(woven["w2"], "w2")
        for t in range(PACK):
            acc = bank(t, [P, S], f"depth_acc{t}")
            product(acc[:], w2_mx, t, two_words[:], two_bytes[:])
            if t == 0:
                first_sig = keep.tile([P, S], F32, name="first_sig")
                nc.scalar.activation(first_sig[:], acc[:], ACT.Sigmoid, scale=-1.0, bias=-math.log(5.0))
                nc.scalar.activation(logits[0][:, :S], first_sig[:], ACT.Copy, bias=0.25)
            else:
                nc.scalar.activation(logits[t][:, :S], acc[:], ACT.Copy, scale=-1.0, bias=-math.log(5.0))

        steps = [(range(4), t, k) for t in range(PACK - 1) for k in range(CORNERS)]
        steps += [(range(2 * h, 2 * h + 2), PACK - 1, k) for h in range(2) for k in range(CORNERS)]
        den = []
        den_sq = [keep.tile([P, 2, 2, P, 2], F32, name=f"den_sq{h}", tag=f"den_sq{h}") for h in range(2)]

        def by_word(acc):
            return acc[:].rearrange("s (u e) p -> s u p e", e=2)

        def add_turned(sums, blocks, t, k, values):
            for place, b in enumerate(blocks):
                nc.tensor.matmul(
                    sums[b][:, t, :],
                    values[:, place * P : (place + 1) * P],
                    ident[:],
                    is_transpose=True,
                    start=(k == 0),
                    stop=(k == CORNERS - 1),
                )

        def square(h):
            for b in range(2):
                nc.scalar.activation(den_sq[h][:, b], by_word(den[2 * h + b]), ACT.Square)

        weights = []
        sigs = []

        def weigh(n):
            blocks, t, k = steps[n]
            width = len(blocks) * P
            offsets = corner_lists[k][:, blocks.start * 8 : blocks.stop * 8]
            weight = keep.tile([P, width], F32, name=f"weight{n}", tag="w1_raw1" if n == 0 else f"weight{n}", align_bytes=64)
            if t == 0:
                nc.vector.tensor_tensor(weight[:], logits[0][:].indirect(offsets), bary[k][:], ALU.mult)
            else:
                if n <= CORNERS + 1:
                    columns = S if n == CORNERS else (2 * CORNERS + 2) * S
                    tag = "early_sig" if n == CORNERS else "gain"
                    sigs.append(keep.tile([P, columns], F32, name=f"sigs{n}", tag=tag, align_bytes=64))
                start = sum(w.shape[1] for w in weights[CORNERS + 1 :])
                sig = sigs[-1][:, start : start + width]
                nc.scalar.activation(sig, logits[t][:].indirect(offsets), ACT.Sigmoid)
                nc.vector.scalar_tensor_tensor(
                    weight[:], sig, 0.25, bary[k][:, blocks.start * P : blocks.stop * P], ALU.add, ALU.mult
                )
            weights.append(weight)
            if n > 0:
                add_turned(den, blocks, t, k, weight)
            if n == len(steps) - 2:
                square(0)

        for half in range(2):
            weave(w1_raw, woven["w1"], half, nc.vector.tensor_copy)
        weigh(0)
        w1_mx = quantise_weight(woven["w1"], "w1")
        for t in range(PACK):
            acc = bank(PACK + t, [P, S], f"attr_acc{t}")
            product(acc[:], w1_mx, t, offs_words[:], offs_bytes[:])
            nc.scalar.activation(attrs[t][:, :S], acc[:], ACT.Copy, scale=gain[:, t : t + 1])
        den += [bank(PACK + b, [P, PACK, P], f"den{b}") for b in range(4)]
        num = [bank(b, [P, PACK, P], f"num{b}") for b in range(4)]
        add_turned(den, *steps[0], weights[0])

        def add_term(n, term):
            blocks, t, k = steps[n]
            offsets = corner_lists[k][:, blocks.start * 8 : blocks.stop * 8]
            nc.vector.tensor_tensor(term, attrs[t][:].indirect(offsets), weights[n][:], ALU.mult)
            add_turned(num, blocks, t, k, term)

        for n in range(len(steps) - CORNERS):
            while len(weights) < len(steps) and sum(w.shape[1] for w in weights) < S * (3 + 2 * n):
                weigh(len(weights))
            term = ring.tile([P, weights[n].shape[1]], F32, name="term")
            add_term(n, term[:])

        den_log = []
        for h in range(2):
            if h == 1:
                square(1)
            tile = keep.tile([P, 2, S], F32, name=f"den_log{h}", tag="logit3" if h == 0 else "den_log1", align_bytes=64)
            nc.scalar.activation(
                tile[:].rearrange("s b c -> s (b c)"), den_sq[h][:].rearrange("s b u p e -> s (b u p e)"), ACT.Ln
            )
            den_log.append(tile)
        inv_sq = []
        for h in range(2):
            if h == 1:
                w3_woven = keep.tile([P, PACK, P, PACK], BF16, name="w3_woven", tag="logit3", align_bytes=64)
                for half in range(2):
                    weave(w3_raw, w3_woven, half, nc.scalar.copy)
            tile = keep.tile([P, 2, 2, P, 2], F32, name=f"inv_sq{h}", tag="den_sq1" if h == 0 else "inv_sq1")
            for b in range(2):
                nc.scalar.activation(
                    tile[:, b].rearrange("s u p e -> s (u p e)"), den_log[h][:, b, :], ACT.Exp, scale=-1.0
                )
            inv_sq.append(tile)


        inv = {}
        z_rows = {}
        z_woven = {}
        results = {}
        sums = {}

        def invert(b):
            tile = keep.tile([P, 2, P, 2], F32, name=f"inv{b}", tag=f"inv{b}")
            nc.vector.tensor_tensor(tile[:], by_word(den[b]), inv_sq[b // 2][:, b % 2], ALU.mult)
            inv[b] = tile

        def divide(b):
            tile = keep.tile([P, 2, P, 2], BF16, name=f"z_rows{b}")
            nc.vector.tensor_tensor(tile[:], by_word(num[b]), inv[b][:], ALU.mult)
            z_rows[b] = tile

        def turn_back(h):
            acc = bank(PACK + 2 * h, [P, 2, 2, P], f"z_acc{h}")
            for b in range(2):
                words = z_rows[2 * h + b][:].rearrange("s u p e -> s (u p e)").bitcast(F32)
                for u in range(2):
                    nc.tensor.transpose(acc[:, b, u, :], words[:, u * P : (u + 1) * P], ident[:])
            tile = keep.tile([P, 2, P, PACK], BF16, name=f"z_woven{h}", tag=f"z_woven{h}", align_bytes=64)
            nc.scalar.copy(
                tile[:].rearrange("p b s j -> p (b s j)").bitcast(F32).rearrange("p (b s u) -> p b s u", b=2, u=2),
                acc[:].rearrange("p b u s -> p b s u"),
            )
            z_woven[h] = tile

        def project(h):
            codes, scales = quantise(z_woven[h][:], f"z_{h}")
            banks = (PACK + 2 * h + 1, 2 * h, 2 * h + 1, PACK + 2 * h)
            for t in range(PACK):
                acc = bank(banks[t], [P, HALF], f"out_acc{h}_{t}")
                product(acc[:], w3_mx, t, codes[:], scales[:])
                sums[h, t] = acc

        def take(h, t):
            tag = "z_woven1" if (h, t) == (0, 1) else f"result{h}_{t}"
            tile = keep.tile([P, HALF], F32, name=f"result{h}_{t}", tag=tag, align_bytes=64)
            nc.scalar.copy(tile[:], sums[h, t][:])
            results[h, t] = tile

        def put(h, t):
            offsets = slot_list[:, h * HALF_COLS : (h + 1) * HALF_COLS]
            nc.vector.tensor_copy(pages[t][:].indirect(offsets), results[h, t][:])
            if h == 1:
                nc.sync.dma_start(out=out.rearrange("(p t) c -> p t c", t=PACK)[:, t, :], in_=pages[t][:])

        invert(0)
        invert(1)
        divide(0)
        divide(1)
        turn_back(0)
        last_terms = keep.tile([P, CORNERS, HALF], F32, name="last_terms", tag="inv1")
        for k in range(CORNERS):
            add_term(len(steps) - CORNERS + k, last_terms[:, k, :])
        w3_mx = quantise_weight(w3_woven, "w3")
        project(0)
        take(0, 0)
        invert(2)
        invert(3)
        divide(2)
        divide(3)
        turn_back(1)
        put(0, 0)
        project(1)
        for t in range(1, PACK):
            take(0, t)
            take(1, t - 1)
        take(1, PACK - 1)
        for t in range(1, PACK):
            put(0, t)
            put(1, t - 1)
        put(1, PACK - 1)
